import numpy as np
import ml_dtypes


def mxq(x, axis, fmt="e4m3"):
    dtype, down = {"e4m3": (ml_dtypes.float8_e4m3fn, 7), "e5m2": (ml_dtypes.float8_e5m2, 14)}[fmt]
    v = np.moveaxis(np.asarray(x, np.float32).astype(ml_dtypes.bfloat16).astype(np.float64), axis, -1)
    blocks = v.reshape(v.shape[:-1] + (-1, 32))
    amax = np.abs(blocks).max(-1, keepdims=True)
    byte = np.maximum(np.where(amax > 0, np.frexp(amax)[1] - 1 + 127, 0) - down, 1)
    scale = np.exp2(byte - 127.0)
    codes = (blocks / scale).astype(np.float32).astype(dtype).astype(np.float64)
    return np.moveaxis((codes * scale).reshape(v.shape), -1, axis)


WIDE = False


def mx_kscale(k):
    if not WIDE:
        return np.ones(k)
    levels = np.array([10, -10, 5, -5, 0])
    if k % 512:
        return np.exp2(np.random.permutation(np.resize(levels, k // 32))).repeat(32)
    a = np.empty((k // 512, 16))
    for p in range(k // 512):
        a[p, :8] = np.random.permutation(np.resize(levels, 8))
        for g in range(8):
            far = levels[np.abs(levels - a[p, g]) >= 10]
            a[p, g + 8] = far[np.random.randint(len(far))]
    return np.exp2(a.ravel()).repeat(32)


BF16 = ml_dtypes.bfloat16


def bf(x):
    return np.asarray(x, np.float32).astype(BF16)


def f64(x):
    return np.asarray(x).astype(np.float64)


E2M1 = np.array([0.0, 0.5, 1.0, 1.5, 2.0, 3.0, 4.0, 6.0, -0.0, -0.5, -1.0, -1.5, -2.0, -3.0, -4.0, -6.0])


def pack_weight(w, fmt):
    k, n = w.shape
    w = f64(bf(w)).reshape(k // 32, 32, n)
    amax = np.abs(w).max(1)
    if fmt == "e4m3":
        byte = np.frexp(amax)[1] - 1 + 127 - 7
    else:
        mant, ex = np.frexp(amax / 6.0)
        byte = np.where(mant > 0.5, ex, ex - 1) + 127
    byte = np.clip(np.where(amax > 0, byte, 1), 1, 254)
    scaled = (w * np.exp2(127.0 - byte)[:, None, :]).reshape(k, n).astype(np.float32)
    by_word = np.ascontiguousarray(scaled.reshape(k // 512, 128, 4, n).transpose(0, 1, 3, 2))
    if fmt == "e4m3":
        words = by_word.astype(ml_dtypes.float8_e4m3fn).view(np.uint8)
    else:
        c = by_word.astype(ml_dtypes.float4_e2m1fn).view(np.uint8) & 0xF
        words = c[..., 0::2] | (c[..., 1::2] << 4)
    return np.ascontiguousarray(words), np.ascontiguousarray(byte.astype(np.uint8).reshape(k // 512, 16, n))


def unpack_weight(words, scales, fmt):
    g, p, n, _ = words.shape
    if fmt == "e4m3":
        vals = np.ascontiguousarray(words).view(ml_dtypes.float8_e4m3fn).astype(np.float64)
    else:
        nib = np.empty((g, p, n, 4), np.uint8)
        nib[..., 0::2] = words & 0xF
        nib[..., 1::2] = words >> 4
        vals = E2M1[nib]
    vals = vals * np.repeat(np.exp2(scales.astype(np.float64) - 127.0), 8, axis=1)[..., None]
    return vals.transpose(0, 1, 3, 2).reshape(g * 512, n)
def pack4(w):
    words, scales = pack_weight(w, "e2m1")
    return words.reshape(words.shape[0], 128, -1), scales


def unpack4(words, scales):
    return unpack_weight(words.reshape(words.shape[0], 128, -1, 2), scales, "e2m1")


S, K1, K2, G = 2048, 512, 1536, 1024


def setup_inputs():
    t1, t2 = mx_kscale(K1), mx_kscale(K2)
    value = 1.5 * np.random.standard_normal((S, G))
    arrive = np.exp(0.5 * np.random.standard_normal(S)) * np.concatenate([t1, t2])
    p_near = np.exp(1.5 * np.random.standard_normal((S, K1)) - 1.125) / (2 * K1) / t1
    p_far = np.exp(np.random.standard_normal((K2, S)) - 0.5) / (2 * K2) / t2[:, None]
    p_far_words, p_far_scales = pack4(p_far)
    return {"value": bf(value),
            "arrive": bf(arrive),
            "p_near": bf(p_near),
            "p_far_words": p_far_words,
            "p_far_scales": p_far_scales,
            "discount": bf(0.8 + 0.05 * np.random.standard_normal(S)),
            "reward": bf(0.5 * np.random.standard_normal((S, G)))}


def reference(value, arrive, p_near, p_far_words, p_far_scales, discount, reward):
    z = np.exp(f64(value)) * f64(arrive)[:, None]
    near = mxq(f64(p_near), 1, "e4m3") @ mxq(z[:K1], 0, "e4m3")
    far = unpack4(p_far_words, p_far_scales).T @ mxq(z[K1:], 0, "e4m3")
    total = near + far
    return f64(discount)[:, None] * np.log(total) + f64(reward)

@@ -1,0 +1,227 @@
+from contextlib import ExitStack
+
+import concourse.mybir as mybir
+from concourse.masks import make_identity
+
+S, K1, K2, G = 2048, 512, 1536, 1024
+FLOPS = 2 * S * S * G
+
+F32 = mybir.dt.float32
+BF16 = mybir.dt.bfloat16
+I32 = mybir.dt.int32
+U32 = mybir.dt.uint32
+U8 = mybir.dt.uint8
+FP8X4 = mybir.dt.float8_e4m3fn_x4
+FP4X4 = mybir.dt.float4_e2m1fn_x4
+EXP = mybir.ActivationFunctionType.Exp
+LN = mybir.ActivationFunctionType.Ln
+ALU = mybir.AluOpType
+
+P = 128
+NG = S // 512
+HALF = 512
+NT = S // P
+FIRST = 7
+TINY = 2.0**-64
+
+
+def tile_soft_value_backup_s1_kernel(tc, value, arrive, p_near, p_far_words, p_far_scales, discount, reward, out):
+    nc = tc.nc
+    with ExitStack() as ctx:
+        ctx.enter_context(tc.manual_schedule())
+        keep = ctx.enter_context(tc.tile_pool(name="keep", bufs=1))
+        zpool = ctx.enter_context(tc.tile_pool(name="zpool", bufs=3))
+        opool = ctx.enter_context(tc.tile_pool(name="opool", bufs=6))
+        psum = ctx.enter_context(tc.psum_pool(name="psum", bufs=8))
+
+        raw = keep.tile([P, 2, 8, 512], BF16, name="raw", align_bytes=64)
+        val = keep.tile([P, 2, NG, 4, HALF], BF16, name="val", align_bytes=64)
+        words = keep.tile([P, 3, 2 * S], U8, name="words", align_bytes=64)
+        fscale = keep.tile([P, 3, S], U8, name="fscale", align_bytes=64)
+        rew = keep.tile([P, NT, G], BF16, name="rew", align_bytes=64)
+        grouped = keep.tile([P, 2, 1024, 4], BF16, name="grouped", align_bytes=64)
+        pcode = keep.tile([P, S], U32, name="pcode", align_bytes=64)
+        pscale = keep.tile([P, S], U8, name="pscale", align_bytes=64)
+        zcode = keep.tile([P, NG, G], U32, name="zcode", align_bytes=64)
+        zscale = keep.tile([P, NG, G], U8, name="zscale", align_bytes=64)
+        ident = keep.tile([P, P], F32, name="ident", align_bytes=64)
+        arr = keep.tile([P, NG, 4], BF16, name="arr")
+        arr_pos = keep.tile([P, NG * 4], F32, name="arr_pos")
+        arr_off = keep.tile([P, NG * 4], F32, name="arr_off")
+        arr_ln = keep.tile([P, NG * 4], F32, name="arr_ln")
+        lna = keep.tile([P, NG * 4], F32, name="lna")
+        warm = keep.tile([P, 2], F32, name="warm")
+        drow = keep.tile([P, P], BF16, name="drow", align_bytes=64)
+        drow32 = keep.tile([P, P], F32, name="drow32", align_bytes=64)
+        disc = keep.tile([P, NT], F32, name="disc")
+
+        def load_near(i):
+            nc.sync.dma_start(
+                out=raw[:, i, :, :],
+                in_=p_near[i * 1024 : (i + 1) * 1024, :].rearrange("(p s) k -> p s k", s=8),
+            )
+
+        def load_value(g, h):
+            nc.sync.dma_start(
+                out=val[:, h, g, :, :],
+                in_=value[g * 512 : (g + 1) * 512, h * HALF : (h + 1) * HALF].rearrange("(p j) w -> p j w", j=4),
+            )
+
+        def load_words(g):
+            nc.sync.dma_start(out=words[:, g - 1, :].bitcast(I32), in_=p_far_words[g - 1].bitcast(I32))
+
+        def load_reward(i):
+            nc.sync.dma_start(
+                out=rew[:, 4 * i : 4 * i + 4, :],
+                in_=reward[i * 512 : (i + 1) * 512, :].rearrange("(m p) w -> p m w", p=P),
+            )
+
+        nc.gpsimd.memset(drow[:], 0.0)
+        nc.scalar.dma_start(out=arr[:], in_=arrive.rearrange("(g p j) -> p g j", p=P, j=4))
+        load_near(0)
+        load_value(0, 0)
+        load_value(1, 0)
+        load_words(1)
+        load_value(2, 0)
+        load_words(2)
+        load_value(3, 0)
+        load_words(3)
+        load_value(0, 1)
+        load_value(1, 1)
+        load_near(1)
+        load_value(2, 1)
+        load_value(3, 1)
+        for i in range(4):
+            load_reward(i)
+
+        nc.vector.memset(warm[:], 1.0)
+        nc.scalar.activation(out=warm[:, 1:2], in_=warm[:, 0:1], func=LN)
+        nc.vector.memset(fscale[:].rearrange("p g n -> p (g n)").bitcast(I32), 0)
+        make_identity(nc, ident[:])
+        nc.scalar.dma_start(out=drow[0:NT, :], in_=discount.rearrange("(m p) -> m p", p=P))
+        for q in range(4):
+            nc.scalar.dma_start(
+                out=fscale[32 * q : 32 * q + 4, :, :].bitcast(I32),
+                in_=p_far_scales[:, 4 * q : 4 * q + 4, :].rearrange("g r n -> r g n").bitcast(I32),
+            )
+
+        flat = arr[:].rearrange("p g j -> p (g j)")
+        nc.vector.tensor_scalar(out=arr_pos[:], in0=flat, scalar1=TINY, scalar2=None, op0=ALU.max)
+        nc.vector.tensor_scalar(out=arr_off[:], in0=flat, scalar1=TINY, scalar2=-256.0, op0=ALU.is_lt, op1=ALU.mult)
+        nc.scalar.activation(out=arr_ln[:], in_=arr_pos[:], func=LN)
+        nc.vector.tensor_tensor(out=lna[:], in0=arr_ln[:], in1=arr_off[:], op=ALU.add)
+
+        def turn_near(i, k):
+            bank = psum.tile([P, 512], F32, name="bank")
+            w = raw[:, i, :, :].rearrange("p s k -> p (s k)").bitcast(F32)
+            for e in range(4):
+                c0 = 256 * (2 * k + e // 2) + e % 2
+                nc.tensor.transpose(bank[:, e * P : (e + 1) * P], w[:, c0 : c0 + 255 : 2], ident[:])
+            gw = grouped[:, i, :, :].rearrange("q n j -> q (n j)").bitcast(F32).rearrange("q (p e) -> q p e", e=16)
+            nc.vector.tensor_copy(out=gw[:, :, 4 * k : 4 * k + 4], in_=bank[:].rearrange("q (e p) -> q p e", e=4))
+
+        def quantize_near(i, c):
+            cols = slice(i * 1024 + c * 512, i * 1024 + (c + 1) * 512)
+            nc.vector.quantize_mx(
+                out=pcode[:, cols].bitcast(FP8X4),
+                scales=pscale[:, cols],
+                in_=grouped[:, i, c * 512 : (c + 1) * 512, :].rearrange("p n j -> p (n j)"),
+            )
+
+        def desirability(g, h, parts):
+            zc = zpool.tile([P, 4, HALF], BF16, name="zc", align_bytes=64)
+            wide = HALF // parts
+            for c in range(parts):
+                cols = slice(c * wide, (c + 1) * wide)
+                for j in range(4):
+                    nc.scalar.activation(
+                        out=zc[:, j, cols], in_=val[:, h, g, j, cols], func=EXP, bias=lna[:, 4 * g + j : 4 * g + j + 1]
+                    )
+            zi = zpool.tile([P, HALF, 4], BF16, name="zi", align_bytes=64)
+            for c in range(2):
+                cols = slice(c * 256, (c + 1) * 256)
+                nc.vector.tensor_copy(out=zi[:, cols, :], in_=zc[:, :, cols].rearrange("p j w -> p w j"))
+            for c in range(2):
+                cols = slice(c * 256, (c + 1) * 256)
+                dst = slice(h * HALF + c * 256, h * HALF + (c + 1) * 256)
+                nc.vector.quantize_mx(
+                    out=zcode[:, g, dst].bitcast(FP8X4),
+                    scales=zscale[:, g, dst],
+                    in_=zi[:, cols, :].rearrange("p w j -> p (w j)"),
+                )
+
+        def one_pass(acc, n, g):
+            h, m = divmod(n, NT)
+            mc = slice(m * P, (m + 1) * P)
+            hc = slice(h * HALF, (h + 1) * HALF)
+            if g == 0:
+                lhsT, lhsT_scale = pcode[:, mc].bitcast(FP8X4), pscale[:, mc]
+            else:
+                lhsT = words[:, g - 1, 2 * m * P : 2 * (m + 1) * P].bitcast(FP4X4)
+                lhsT_scale = fscale[:, g - 1, mc]
+            nc.tensor.matmul_mx(
+                out=acc[:],
+                lhsT=lhsT,
+                lhsT_scale=lhsT_scale,
+                rhs=zcode[:, g, hc].bitcast(FP8X4),
+                rhs_scale=zscale[:, g, hc],
+                start=(g == 0),
+                stop=(g == NG - 1),
+            )
+
+        accs = {}
+
+        def open_tile(n):
+            bank = psum.tile([P, 512], F32, name="bank")
+            accs[n] = bank
+
+        def whole_tile(n):
+            open_tile(n)
+            for g in range(NG):
+                one_pass(accs[n], n, g)
+
+        def drain(n):
+            h, m = divmod(n, NT)
+            hc = slice(h * HALF, (h + 1) * HALF)
+            lnt = opool.tile([P, HALF], F32, name="lnt", align_bytes=64)
+            nc.scalar.activation(out=lnt[:], in_=accs[n][:], func=LN)
+            res = opool.tile([P, HALF], F32, name="res", align_bytes=64)
+            nc.vector.scalar_tensor_tensor(
+                out=res[:], in0=lnt[:], scalar=disc[:, m : m + 1], in1=rew[:, m, hc], op0=ALU.mult, op1=ALU.add
+            )
+            nc.sync.dma_start(out=out[m * P : (m + 1) * P, hc], in_=res[:])
+
+        nc.vector.tensor_copy(out=drow32[:], in_=drow[:])
+        dbank = psum.tile([P, 512], F32, name="bank")
+        nc.tensor.transpose(dbank[:, 0:P], drow32[:], ident[:])
+        nc.vector.tensor_copy(out=disc[:], in_=dbank[:, 0:NT])
+
+        for k in range(4):
+            turn_near(0, k)
+        quantize_near(0, 0)
+        quantize_near(0, 1)
+
+        for n in range(FIRST):
+            open_tile(n)
+        for g in range(NG):
+            desirability(g, 0, 2 if g == 0 else 1)
+            for n in range(FIRST):
+                one_pass(accs[n], n, g)
+        desirability(0, 1, 1)
+
+        for k in range(4):
+            drain(k)
+            turn_near(1, k)
+        quantize_near(1, 0)
+        quantize_near(1, 1)
+        for n in range(FIRST, NT):
+            if n - 3 <= FIRST:
+                drain(n - 3)
+            whole_tile(n)
+        for g in range(1, NG):
+            desirability(g, 1, 1)
+        for n in range(NT, 2 * NT):
+            drain(n - 8)
+            whole_tile(n)
+        for n in range(2 * NT - 8, 2 * NT):
+            drain(n)

@@ -31,11 +31,12 @@ def tile_soft_value_backup_s1_kernel(tc, value, arrive, p_near, p_far_words, p_f
         ctx.enter_context(tc.manual_schedule())
         keep = ctx.enter_context(tc.tile_pool(name="keep", bufs=1))
         zpool = ctx.enter_context(tc.tile_pool(name="zpool", bufs=3))
+        rpool = ctx.enter_context(tc.tile_pool(name="rpool", bufs=4))
         opool = ctx.enter_context(tc.tile_pool(name="opool", bufs=6))
         psum = ctx.enter_context(tc.psum_pool(name="psum", bufs=8))
 
         raw = keep.tile([P, 2, 8, 512], BF16, name="raw", align_bytes=64)
-        val = keep.tile([P, 2, NG, 4, HALF], BF16, name="val", align_bytes=64)
+        val = keep.tile([P, NG, 4, G], BF16, name="val", align_bytes=64)
         words = keep.tile([P, 3, 2 * S], U8, name="words", align_bytes=64)
         fscale = keep.tile([P, 3, S], U8, name="fscale", align_bytes=64)
         rew = keep.tile([P, NT, G], BF16, name="rew", align_bytes=64)
@@ -55,16 +56,16 @@ def tile_soft_value_backup_s1_kernel(tc, value, arrive, p_near, p_far_words, p_f
         drow32 = keep.tile([P, P], F32, name="drow32", align_bytes=64)
         disc = keep.tile([P, NT], F32, name="disc")
 
-        def load_near(i):
+        def load_near(i, s0, s1):
             nc.sync.dma_start(
-                out=raw[:, i, :, :],
-                in_=p_near[i * 1024 : (i + 1) * 1024, :].rearrange("(p s) k -> p s k", s=8),
+                out=raw[:, i, s0:s1, :],
+                in_=p_near[i * 1024 : (i + 1) * 1024, :].rearrange("(p s) k -> p s k", s=8)[:, s0:s1, :],
             )
 
-        def load_value(g, h):
+        def load_value(g, c0, c1):
             nc.sync.dma_start(
-                out=val[:, h, g, :, :],
-                in_=value[g * 512 : (g + 1) * 512, h * HALF : (h + 1) * HALF].rearrange("(p j) w -> p j w", j=4),
+                out=val[:, g, :, c0:c1],
+                in_=value[g * 512 : (g + 1) * 512, c0:c1].rearrange("(p j) w -> p j w", j=4),
             )
 
         def load_words(g):
@@ -77,33 +78,34 @@ def tile_soft_value_backup_s1_kernel(tc, value, arrive, p_near, p_far_words, p_f
             )
 
         nc.gpsimd.memset(drow[:], 0.0)
-        nc.scalar.dma_start(out=arr[:], in_=arrive.rearrange("(g p j) -> p g j", p=P, j=4))
-        load_near(0)
-        load_value(0, 0)
-        load_value(1, 0)
-        load_words(1)
-        load_value(2, 0)
-        load_words(2)
-        load_value(3, 0)
-        load_words(3)
-        load_value(0, 1)
-        load_value(1, 1)
-        load_near(1)
-        load_value(2, 1)
-        load_value(3, 1)
-        for i in range(4):
-            load_reward(i)
-
         nc.vector.memset(warm[:], 1.0)
-        nc.scalar.activation(out=warm[:, 1:2], in_=warm[:, 0:1], func=LN)
         nc.vector.memset(fscale[:].rearrange("p g n -> p (g n)").bitcast(I32), 0)
-        make_identity(nc, ident[:])
+        nc.scalar.dma_start(out=arr[:], in_=arrive.rearrange("(g p j) -> p g j", p=P, j=4))
+        nc.scalar.activation(out=warm[:, 1:2], in_=warm[:, 0:1], func=LN)
         nc.scalar.dma_start(out=drow[0:NT, :], in_=discount.rearrange("(m p) -> m p", p=P))
         for q in range(4):
             nc.scalar.dma_start(
                 out=fscale[32 * q : 32 * q + 4, :, :].bitcast(I32),
                 in_=p_far_scales[:, 4 * q : 4 * q + 4, :].rearrange("g r n -> r g n").bitcast(I32),
             )
+        load_near(0, 0, 4)
+        load_near(0, 4, 8)
+        load_value(0, 0, HALF)
+        load_value(1, 0, HALF)
+        load_words(1)
+        load_value(2, 0, G)
+        load_value(3, 0, HALF)
+        load_words(2)
+        load_value(0, HALF, G)
+        load_words(3)
+        load_near(1, 0, 8)
+        load_reward(0)
+        load_value(1, HALF, G)
+        load_value(3, HALF, G)
+        for i in range(1, 4):
+            load_reward(i)
+
+        make_identity(nc, ident[:])
 
         flat = arr[:].rearrange("p g j -> p (g j)")
         nc.vector.tensor_scalar(out=arr_pos[:], in0=flat, scalar1=TINY, scalar2=None, op0=ALU.max)
@@ -135,12 +137,15 @@ def tile_soft_value_backup_s1_kernel(tc, value, arrive, p_near, p_far_words, p_f
                 cols = slice(c * wide, (c + 1) * wide)
                 for j in range(4):
                     nc.scalar.activation(
-                        out=zc[:, j, cols], in_=val[:, h, g, j, cols], func=EXP, bias=lna[:, 4 * g + j : 4 * g + j + 1]
+                        out=zc[:, j, cols], in_=val[:, g, j, h * HALF + c * wide : h * HALF + (c + 1) * wide], func=EXP, bias=lna[:, 4 * g + j : 4 * g + j + 1]
                     )
             zi = zpool.tile([P, HALF, 4], BF16, name="zi", align_bytes=64)
             for c in range(2):
                 cols = slice(c * 256, (c + 1) * 256)
-                nc.vector.tensor_copy(out=zi[:, cols, :], in_=zc[:, :, cols].rearrange("p j w -> p w j"))
+                nc.vector.tensor_copy(
+                    out=zi[:, cols, :].rearrange("p (c i) j -> p c j i", i=4),
+                    in_=zc[:, :, cols].rearrange("p j (c i) -> p c j i", i=4),
+                )
             for c in range(2):
                 cols = slice(c * 256, (c + 1) * 256)
                 dst = slice(h * HALF + c * 256, h * HALF + (c + 1) * 256)
@@ -150,46 +155,70 @@ def tile_soft_value_backup_s1_kernel(tc, value, arrive, p_near, p_far_words, p_f
                     in_=zi[:, cols, :].rearrange("p w j -> p (w j)"),
                 )
 
-        def one_pass(acc, n, g):
+        NEAR_FIRST = (0, 1, 2, 3)
+        NEAR_LAST = (1, 2, 3, 0)
+
+        def one_pass(n, order, i, c0=0, width=HALF):
             h, m = divmod(n, NT)
+            g = order[i]
             mc = slice(m * P, (m + 1) * P)
-            hc = slice(h * HALF, (h + 1) * HALF)
+            zc = slice(h * HALF + c0, h * HALF + c0 + width)
             if g == 0:
                 lhsT, lhsT_scale = pcode[:, mc].bitcast(FP8X4), pscale[:, mc]
             else:
                 lhsT = words[:, g - 1, 2 * m * P : 2 * (m + 1) * P].bitcast(FP4X4)
                 lhsT_scale = fscale[:, g - 1, mc]
             nc.tensor.matmul_mx(
-                out=acc[:],
+                out=sums[n][:, c0 : c0 + width],
                 lhsT=lhsT,
                 lhsT_scale=lhsT_scale,
-                rhs=zcode[:, g, hc].bitcast(FP8X4),
-                rhs_scale=zscale[:, g, hc],
-                start=(g == 0),
-                stop=(g == NG - 1),
+                rhs=zcode[:, g, zc].bitcast(FP8X4),
+                rhs_scale=zscale[:, g, zc],
+                start=(i == 0),
+                stop=(i == NG - 1),
             )
 
-        accs = {}
+        sums = {}
 
         def open_tile(n):
             bank = psum.tile([P, 512], F32, name="bank")
-            accs[n] = bank
+            sums[n] = bank
 
-        def whole_tile(n):
+        def whole_tile(n, order, parts=1):
             open_tile(n)
-            for g in range(NG):
-                one_pass(accs[n], n, g)
+            width = HALF // parts
+            for c in range(parts):
+                for i in range(NG):
+                    one_pass(n, order, i, c * width, width)
+
+        def set_aside(n):
+            rest = rpool.tile([P, HALF], F32, name="rest", align_bytes=64)
+            nc.vector.tensor_copy(out=rest[:], in_=sums[n][:])
+            sums[n] = rest
+
+        logs = {}
+
+        def log_part(n, c0=0, width=HALF):
+            if c0 == 0:
+                lnt = opool.tile([P, HALF], F32, name="lnt", align_bytes=64)
+                logs[n] = lnt
+            nc.scalar.activation(out=logs[n][:, c0 : c0 + width], in_=sums[n][:, c0 : c0 + width], func=LN)
+
+        def finish(n, parts=1):
+            h, m = divmod(n, NT)
+            res = opool.tile([P, HALF], F32, name="res", align_bytes=64)
+            width = HALF // parts
+            for c in range(parts):
+                cols = slice(c * width, (c + 1) * width)
+                oc = slice(h * HALF + c * width, h * HALF + (c + 1) * width)
+                nc.vector.scalar_tensor_tensor(
+                    out=res[:, cols], in0=logs[n][:, cols], scalar=disc[:, m : m + 1], in1=rew[:, m, oc], op0=ALU.mult, op1=ALU.add
+                )
+                nc.sync.dma_start(out=out[m * P : (m + 1) * P, oc], in_=res[:, cols])
 
         def drain(n):
-            h, m = divmod(n, NT)
-            hc = slice(h * HALF, (h + 1) * HALF)
-            lnt = opool.tile([P, HALF], F32, name="lnt", align_bytes=64)
-            nc.scalar.activation(out=lnt[:], in_=accs[n][:], func=LN)
-            res = opool.tile([P, HALF], F32, name="res", align_bytes=64)
-            nc.vector.scalar_tensor_tensor(
-                out=res[:], in0=lnt[:], scalar=disc[:, m : m + 1], in1=rew[:, m, hc], op0=ALU.mult, op1=ALU.add
-            )
-            nc.sync.dma_start(out=out[m * P : (m + 1) * P, hc], in_=res[:])
+            log_part(n)
+            finish(n)
 
         nc.vector.tensor_copy(out=drow32[:], in_=drow[:])
         dbank = psum.tile([P, 512], F32, name="bank")
@@ -199,29 +228,47 @@ def tile_soft_value_backup_s1_kernel(tc, value, arrive, p_near, p_far_words, p_f
         for k in range(4):
             turn_near(0, k)
         quantize_near(0, 0)
-        quantize_near(0, 1)
 
         for n in range(FIRST):
             open_tile(n)
         for g in range(NG):
             desirability(g, 0, 2 if g == 0 else 1)
+            if g == 0:
+                quantize_near(0, 1)
             for n in range(FIRST):
-                one_pass(accs[n], n, g)
+                one_pass(n, NEAR_FIRST, g)
         desirability(0, 1, 1)
 
         for k in range(4):
-            drain(k)
             turn_near(1, k)
+            log_part(k)
         quantize_near(1, 0)
         quantize_near(1, 1)
+        for n in range(4):
+            finish(n)
         for n in range(FIRST, NT):
-            if n - 3 <= FIRST:
-                drain(n - 3)
-            whole_tile(n)
+            if n in (FIRST + 1, FIRST + 2, FIRST + 3, NT - 1):
+                drain(min(n - 4, FIRST))
+            whole_tile(n, NEAR_LAST)
         for g in range(1, NG):
             desirability(g, 1, 1)
-        for n in range(NT, 2 * NT):
-            drain(n - 8)
-            whole_tile(n)
-        for n in range(2 * NT - 8, 2 * NT):
+            for n in {1: (8,), 2: (9, 10), 3: (11,)}[g]:
+                set_aside(n)
+        for n in range(NT, NT + 3):
+            open_tile(n)
+        for g in range(NG):
+            for n in range(NT, NT + 3):
+                one_pass(n, NEAR_FIRST, g)
+        for n in range(8, 11):
             drain(n)
+        LAST = 2 * NT - 1
+        for n in range(NT + 3, LAST):
+            drain(n - 8)
+            whole_tile(n, NEAR_FIRST)
+        drain(LAST - 8)
+        whole_tile(LAST, NEAR_FIRST, 4)
+        for n in range(LAST - 7, LAST):
+            drain(n)
+        for c in range(4):
+            log_part(LAST, c * P, P)
+        finish(LAST, 4)

@@ -30,36 +30,38 @@ def tile_soft_value_backup_s1_kernel(tc, value, arrive, p_near, p_far_words, p_f
     with ExitStack() as ctx:
         ctx.enter_context(tc.manual_schedule())
         keep = ctx.enter_context(tc.tile_pool(name="keep", bufs=1))
+        epool = ctx.enter_context(tc.tile_pool(name="epool", bufs=4))
         zpool = ctx.enter_context(tc.tile_pool(name="zpool", bufs=3))
-        rpool = ctx.enter_context(tc.tile_pool(name="rpool", bufs=4))
-        opool = ctx.enter_context(tc.tile_pool(name="opool", bufs=6))
+        rpool = ctx.enter_context(tc.tile_pool(name="rpool", bufs=FIRST))
+        lpool = ctx.enter_context(tc.tile_pool(name="lpool", bufs=5))
+        opool = ctx.enter_context(tc.tile_pool(name="opool", bufs=14))
         psum = ctx.enter_context(tc.psum_pool(name="psum", bufs=8))
 
-        raw = keep.tile([P, 2, 8, 512], BF16, name="raw", align_bytes=64)
+        raw = keep.tile([P, 4, 4, 512], BF16, name="raw", align_bytes=64)
         val = keep.tile([P, NG, 4, G], BF16, name="val", align_bytes=64)
         words = keep.tile([P, 3, 2 * S], U8, name="words", align_bytes=64)
         fscale = keep.tile([P, 3, S], U8, name="fscale", align_bytes=64)
         rew = keep.tile([P, NT, G], BF16, name="rew", align_bytes=64)
-        grouped = keep.tile([P, 2, 1024, 4], BF16, name="grouped", align_bytes=64)
+        grouped = keep.tile([P, 4, 512, 4], BF16, name="grouped", align_bytes=64)
         pcode = keep.tile([P, S], U32, name="pcode", align_bytes=64)
         pscale = keep.tile([P, S], U8, name="pscale", align_bytes=64)
         zcode = keep.tile([P, NG, G], U32, name="zcode", align_bytes=64)
         zscale = keep.tile([P, NG, G], U8, name="zscale", align_bytes=64)
         ident = keep.tile([P, P], F32, name="ident", align_bytes=64)
-        arr = keep.tile([P, NG, 4], BF16, name="arr")
         arr_pos = keep.tile([P, NG * 4], F32, name="arr_pos")
         arr_off = keep.tile([P, NG * 4], F32, name="arr_off")
         arr_ln = keep.tile([P, NG * 4], F32, name="arr_ln")
         lna = keep.tile([P, NG * 4], F32, name="lna")
         warm = keep.tile([P, 2], F32, name="warm")
-        drow = keep.tile([P, P], BF16, name="drow", align_bytes=64)
-        drow32 = keep.tile([P, P], F32, name="drow32", align_bytes=64)
+        arr = keep.tile([P, NG, 4], BF16, name="arr")
+        rows = keep.tile([P, P], BF16, name="rows", align_bytes=64)
+        rows32 = keep.tile([P, P], F32, name="rows32", align_bytes=64)
         disc = keep.tile([P, NT], F32, name="disc")
 
-        def load_near(i, s0, s1):
+        def load_near(q):
             nc.sync.dma_start(
-                out=raw[:, i, s0:s1, :],
-                in_=p_near[i * 1024 : (i + 1) * 1024, :].rearrange("(p s) k -> p s k", s=8)[:, s0:s1, :],
+                out=raw[:, q, :, :],
+                in_=p_near[q * 512 : (q + 1) * 512, :].rearrange("(p s) k -> p s k", s=4),
             )
 
         def load_value(g, c0, c1):
@@ -77,32 +79,33 @@ def tile_soft_value_backup_s1_kernel(tc, value, arrive, p_near, p_far_words, p_f
                 in_=reward[i * 512 : (i + 1) * 512, :].rearrange("(m p) w -> p m w", p=P),
             )
 
-        nc.gpsimd.memset(drow[:], 0.0)
+        nc.vector.memset(rows32[:], 0.0)
+        nc.scalar.dma_start(out=arr[:], in_=arrive.rearrange("(g p j) -> p g j", p=P, j=4))
+        nc.scalar.dma_start(out=rows[0:NT, :], in_=discount.rearrange("(m p) -> m p", p=P))
         nc.vector.memset(warm[:], 1.0)
         nc.vector.memset(fscale[:].rearrange("p g n -> p (g n)").bitcast(I32), 0)
-        nc.scalar.dma_start(out=arr[:], in_=arrive.rearrange("(g p j) -> p g j", p=P, j=4))
         nc.scalar.activation(out=warm[:, 1:2], in_=warm[:, 0:1], func=LN)
-        nc.scalar.dma_start(out=drow[0:NT, :], in_=discount.rearrange("(m p) -> m p", p=P))
+        load_near(0)
+        load_value(0, 0, HALF)
+        load_value(1, 0, HALF)
+        load_near(1)
+        load_words(1)
+        load_value(2, 0, HALF)
         for q in range(4):
-            nc.scalar.dma_start(
+            nc.sync.dma_start(
                 out=fscale[32 * q : 32 * q + 4, :, :].bitcast(I32),
                 in_=p_far_scales[:, 4 * q : 4 * q + 4, :].rearrange("g r n -> r g n").bitcast(I32),
             )
-        load_near(0, 0, 4)
-        load_near(0, 4, 8)
-        load_value(0, 0, HALF)
-        load_value(1, 0, HALF)
-        load_words(1)
-        load_value(2, 0, G)
         load_value(3, 0, HALF)
         load_words(2)
-        load_value(0, HALF, G)
         load_words(3)
-        load_near(1, 0, 8)
-        load_reward(0)
+        load_value(0, HALF, G)
+        load_near(2)
         load_value(1, HALF, G)
+        load_near(3)
+        load_value(2, HALF, G)
         load_value(3, HALF, G)
-        for i in range(1, 4):
+        for i in range(4):
             load_reward(i)
 
         make_identity(nc, ident[:])
@@ -111,27 +114,33 @@ def tile_soft_value_backup_s1_kernel(tc, value, arrive, p_near, p_far_words, p_f
         nc.vector.tensor_scalar(out=arr_pos[:], in0=flat, scalar1=TINY, scalar2=None, op0=ALU.max)
         nc.vector.tensor_scalar(out=arr_off[:], in0=flat, scalar1=TINY, scalar2=-256.0, op0=ALU.is_lt, op1=ALU.mult)
         nc.scalar.activation(out=arr_ln[:], in_=arr_pos[:], func=LN)
+        nc.vector.tensor_copy(out=rows32[0:NT, :], in_=rows[0:NT, :])
+        dbank = psum.tile([P, 512], F32, name="bank")
+        nc.tensor.transpose(dbank[:, 0:P], rows32[:], ident[:])
         nc.vector.tensor_tensor(out=lna[:], in0=arr_ln[:], in1=arr_off[:], op=ALU.add)
 
-        def turn_near(i, k):
+        def turn_near(q, k):
             bank = psum.tile([P, 512], F32, name="bank")
-            w = raw[:, i, :, :].rearrange("p s k -> p (s k)").bitcast(F32)
+            w = raw[:, q, :, :].rearrange("p s k -> p (s k)").bitcast(F32)
             for e in range(4):
                 c0 = 256 * (2 * k + e // 2) + e % 2
                 nc.tensor.transpose(bank[:, e * P : (e + 1) * P], w[:, c0 : c0 + 255 : 2], ident[:])
-            gw = grouped[:, i, :, :].rearrange("q n j -> q (n j)").bitcast(F32).rearrange("q (p e) -> q p e", e=16)
+            return bank
+
+        def group_near(q, k, bank):
+            gw = grouped[:, q, :, :].rearrange("q n j -> q (n j)").bitcast(F32).rearrange("q (p e) -> q p e", e=8)
             nc.vector.tensor_copy(out=gw[:, :, 4 * k : 4 * k + 4], in_=bank[:].rearrange("q (e p) -> q p e", e=4))
 
-        def quantize_near(i, c):
-            cols = slice(i * 1024 + c * 512, i * 1024 + (c + 1) * 512)
+        def quantize_near(q):
+            cols = slice(q * 512, (q + 1) * 512)
             nc.vector.quantize_mx(
                 out=pcode[:, cols].bitcast(FP8X4),
                 scales=pscale[:, cols],
-                in_=grouped[:, i, c * 512 : (c + 1) * 512, :].rearrange("p n j -> p (n j)"),
+                in_=grouped[:, q, :, :].rearrange("p n j -> p (n j)"),
             )
 
         def desirability(g, h, parts):
-            zc = zpool.tile([P, 4, HALF], BF16, name="zc", align_bytes=64)
+            zc = epool.tile([P, 4, HALF], BF16, name="zc", align_bytes=64)
             wide = HALF // parts
             for c in range(parts):
                 cols = slice(c * wide, (c + 1) * wide)
@@ -200,7 +209,7 @@ def tile_soft_value_backup_s1_kernel(tc, value, arrive, p_near, p_far_words, p_f
 
         def log_part(n, c0=0, width=HALF):
             if c0 == 0:
-                lnt = opool.tile([P, HALF], F32, name="lnt", align_bytes=64)
+                lnt = lpool.tile([P, HALF], F32, name="lnt", align_bytes=64)
                 logs[n] = lnt
             nc.scalar.activation(out=logs[n][:, c0 : c0 + width], in_=sums[n][:, c0 : c0 + width], func=LN)
 
@@ -220,53 +229,50 @@ def tile_soft_value_backup_s1_kernel(tc, value, arrive, p_near, p_far_words, p_f
             log_part(n)
             finish(n)
 
-        nc.vector.tensor_copy(out=drow32[:], in_=drow[:])
-        dbank = psum.tile([P, 512], F32, name="bank")
-        nc.tensor.transpose(dbank[:, 0:P], drow32[:], ident[:])
+        turned = [turn_near(q, k) for q in range(2) for k in range(2)]
         nc.vector.tensor_copy(out=disc[:], in_=dbank[:, 0:NT])
+        for k in range(2):
+            group_near(0, k, turned[k])
+        quantize_near(0)
 
-        for k in range(4):
-            turn_near(0, k)
-        quantize_near(0, 0)
-
-        for n in range(FIRST):
+        for n in range(4):
             open_tile(n)
-        for g in range(NG):
-            desirability(g, 0, 2 if g == 0 else 1)
-            if g == 0:
-                quantize_near(0, 1)
+        desirability(0, 0, 2)
+        for n in range(4):
+            one_pass(n, NEAR_FIRST, 0)
+        for k in range(2):
+            group_near(1, k, turned[2 + k])
+        quantize_near(1)
+        for n in range(4, FIRST):
+            open_tile(n)
+            one_pass(n, NEAR_FIRST, 0)
+        for g in range(1, NG):
+            desirability(g, 0, 1)
             for n in range(FIRST):
                 one_pass(n, NEAR_FIRST, g)
-        desirability(0, 1, 1)
 
-        for k in range(4):
-            turn_near(1, k)
-            log_part(k)
-        quantize_near(1, 0)
-        quantize_near(1, 1)
-        for n in range(4):
-            finish(n)
-        for n in range(FIRST, NT):
-            if n in (FIRST + 1, FIRST + 2, FIRST + 3, NT - 1):
-                drain(min(n - 4, FIRST))
+        for n in range(FIRST):
+            set_aside(n)
+        for q in (2, 3):
+            turned = [turn_near(q, k) for k in range(2)]
+            for k in range(2):
+                group_near(q, k, turned[k])
+            quantize_near(q)
+            if q == 2:
+                whole_tile(FIRST, NEAR_LAST)
+        for n in range(FIRST + 1, 13):
             whole_tile(n, NEAR_LAST)
-        for g in range(1, NG):
-            desirability(g, 1, 1)
-            for n in {1: (8,), 2: (9, 10), 3: (11,)}[g]:
-                set_aside(n)
-        for n in range(NT, NT + 3):
-            open_tile(n)
         for g in range(NG):
-            for n in range(NT, NT + 3):
-                one_pass(n, NEAR_FIRST, g)
-        for n in range(8, 11):
-            drain(n)
+            desirability(g, 1, 1)
+        drain(7)
+        for n in range(13, NT):
+            whole_tile(n, NEAR_LAST)
         LAST = 2 * NT - 1
-        for n in range(NT + 3, LAST):
+        for n in range(NT, 2 * NT):
+            if n - NT < FIRST:
+                drain(n - NT)
             drain(n - 8)
-            whole_tile(n, NEAR_FIRST)
-        drain(LAST - 8)
-        whole_tile(LAST, NEAR_FIRST, 4)
+            whole_tile(n, NEAR_FIRST, 4 if n == LAST else 1)
         for n in range(LAST - 7, LAST):
             drain(n)
         for c in range(4):

from contextlib import ExitStack

import concourse.mybir as mybir
from concourse.masks import make_identity

S, K1, K2, G = 2048, 512, 1536, 1024
FLOPS = 2 * S * S * G

F32 = mybir.dt.float32
BF16 = mybir.dt.bfloat16
I32 = mybir.dt.int32
U32 = mybir.dt.uint32
U8 = mybir.dt.uint8
FP8X4 = mybir.dt.float8_e4m3fn_x4
FP4X4 = mybir.dt.float4_e2m1fn_x4
EXP = mybir.ActivationFunctionType.Exp
LN = mybir.ActivationFunctionType.Ln
ALU = mybir.AluOpType

P = 128
NG = S // 512
HALF = 512
NT = S // P
FIRST = 7
TINY = 2.0**-64


def tile_soft_value_backup_s1_kernel(tc, value, arrive, p_near, p_far_words, p_far_scales, discount, reward, out):
    nc = tc.nc
    with ExitStack() as ctx:
        ctx.enter_context(tc.manual_schedule())
        keep = ctx.enter_context(tc.tile_pool(name="keep", bufs=1))
        epool = ctx.enter_context(tc.tile_pool(name="epool", bufs=4))
        zpool = ctx.enter_context(tc.tile_pool(name="zpool", bufs=3))
        rpool = ctx.enter_context(tc.tile_pool(name="rpool", bufs=FIRST))
        lpool = ctx.enter_context(tc.tile_pool(name="lpool", bufs=5))
        opool = ctx.enter_context(tc.tile_pool(name="opool", bufs=14))
        psum = ctx.enter_context(tc.psum_pool(name="psum", bufs=8))

        raw = keep.tile([P, 4, 4, 512], BF16, name="raw", align_bytes=64)
        val = keep.tile([P, NG, 4, G], BF16, name="val", align_bytes=64)
        words = keep.tile([P, 3, 2 * S], U8, name="words", align_bytes=64)
        fscale = keep.tile([P, 3, S], U8, name="fscale", align_bytes=64)
        rew = keep.tile([P, NT, G], BF16, name="rew", align_bytes=64)
        grouped = keep.tile([P, 4, 512, 4], BF16, name="grouped", align_bytes=64)
        pcode = keep.tile([P, S], U32, name="pcode", align_bytes=64)
        pscale = keep.tile([P, S], U8, name="pscale", align_bytes=64)
        zcode = keep.tile([P, NG, G], U32, name="zcode", align_bytes=64)
        zscale = keep.tile([P, NG, G], U8, name="zscale", align_bytes=64)
        ident = keep.tile([P, P], F32, name="ident", align_bytes=64)
        arr_pos = keep.tile([P, NG * 4], F32, name="arr_pos")
        arr_off = keep.tile([P, NG * 4], F32, name="arr_off")
        arr_ln = keep.tile([P, NG * 4], F32, name="arr_ln")
        lna = keep.tile([P, NG * 4], F32, name="lna")
        warm = keep.tile([P, 2], F32, name="warm")
        arr = keep.tile([P, NG, 4], BF16, name="arr")
        rows = keep.tile([P, P], BF16, name="rows", align_bytes=64)
        rows32 = keep.tile([P, P], F32, name="rows32", align_bytes=64)
        disc = keep.tile([P, NT], F32, name="disc")

        def load_near(q):
            nc.sync.dma_start(
                out=raw[:, q, :, :],
                in_=p_near[q * 512 : (q + 1) * 512, :].rearrange("(p s) k -> p s k", s=4),
            )

        def load_value(g, c0, c1):
            nc.sync.dma_start(
                out=val[:, g, :, c0:c1],
                in_=value[g * 512 : (g + 1) * 512, c0:c1].rearrange("(p j) w -> p j w", j=4),
            )

        def load_words(g):
            nc.sync.dma_start(out=words[:, g - 1, :].bitcast(I32), in_=p_far_words[g - 1].bitcast(I32))

        def load_reward(i):
            nc.sync.dma_start(
                out=rew[:, 4 * i : 4 * i + 4, :],
                in_=reward[i * 512 : (i + 1) * 512, :].rearrange("(m p) w -> p m w", p=P),
            )

        nc.vector.memset(rows32[:], 0.0)
        nc.scalar.dma_start(out=arr[:], in_=arrive.rearrange("(g p j) -> p g j", p=P, j=4))
        nc.scalar.dma_start(out=rows[0:NT, :], in_=discount.rearrange("(m p) -> m p", p=P))
        nc.vector.memset(warm[:], 1.0)
        nc.vector.memset(fscale[:].rearrange("p g n -> p (g n)").bitcast(I32), 0)
        nc.scalar.activation(out=warm[:, 1:2], in_=warm[:, 0:1], func=LN)
        load_near(0)
        load_value(0, 0, HALF)
        load_value(1, 0, HALF)
        load_near(1)
        load_words(1)
        load_value(2, 0, HALF)
        for q in range(4):
            nc.sync.dma_start(
                out=fscale[32 * q : 32 * q + 4, :, :].bitcast(I32),
                in_=p_far_scales[:, 4 * q : 4 * q + 4, :].rearrange("g r n -> r g n").bitcast(I32),
            )
        load_value(3, 0, HALF)
        load_words(2)
        load_words(3)
        load_value(0, HALF, G)
        load_near(2)
        load_value(1, HALF, G)
        load_near(3)
        load_value(2, HALF, G)
        load_value(3, HALF, G)
        for i in range(4):
            load_reward(i)

        make_identity(nc, ident[:])

        flat = arr[:].rearrange("p g j -> p (g j)")
        nc.vector.tensor_scalar(out=arr_pos[:], in0=flat, scalar1=TINY, scalar2=None, op0=ALU.max)
        nc.vector.tensor_scalar(out=arr_off[:], in0=flat, scalar1=TINY, scalar2=-256.0, op0=ALU.is_lt, op1=ALU.mult)
        nc.scalar.activation(out=arr_ln[:], in_=arr_pos[:], func=LN)
        nc.vector.tensor_copy(out=rows32[0:NT, :], in_=rows[0:NT, :])
        dbank = psum.tile([P, 512], F32, name="bank")
        nc.tensor.transpose(dbank[:, 0:P], rows32[:], ident[:])
        nc.vector.tensor_tensor(out=lna[:], in0=arr_ln[:], in1=arr_off[:], op=ALU.add)

        def turn_near(q, k):
            bank = psum.tile([P, 512], F32, name="bank")
            w = raw[:, q, :, :].rearrange("p s k -> p (s k)").bitcast(F32)
            for e in range(4):
                c0 = 256 * (2 * k + e // 2) + e % 2
                nc.tensor.transpose(bank[:, e * P : (e + 1) * P], w[:, c0 : c0 + 255 : 2], ident[:])
            return bank

        def group_near(q, k, bank):
            gw = grouped[:, q, :, :].rearrange("q n j -> q (n j)").bitcast(F32).rearrange("q (p e) -> q p e", e=8)
            nc.vector.tensor_copy(out=gw[:, :, 4 * k : 4 * k + 4], in_=bank[:].rearrange("q (e p) -> q p e", e=4))

        def quantize_near(q):
            cols = slice(q * 512, (q + 1) * 512)
            nc.vector.quantize_mx(
                out=pcode[:, cols].bitcast(FP8X4),
                scales=pscale[:, cols],
                in_=grouped[:, q, :, :].rearrange("p n j -> p (n j)"),
            )

        def desirability(g, h, parts):
            zc = epool.tile([P, 4, HALF], BF16, name="zc", align_bytes=64)
            wide = HALF // parts
            for c in range(parts):
                cols = slice(c * wide, (c + 1) * wide)
                for j in range(4):
                    nc.scalar.activation(
                        out=zc[:, j, cols], in_=val[:, g, j, h * HALF + c * wide : h * HALF + (c + 1) * wide], func=EXP, bias=lna[:, 4 * g + j : 4 * g + j + 1]
                    )
            zi = zpool.tile([P, HALF, 4], BF16, name="zi", align_bytes=64)
            for c in range(2):
                cols = slice(c * 256, (c + 1) * 256)
                nc.vector.tensor_copy(
                    out=zi[:, cols, :].rearrange("p (c i) j -> p c j i", i=4),
                    in_=zc[:, :, cols].rearrange("p j (c i) -> p c j i", i=4),
                )
            for c in range(2):
                cols = slice(c * 256, (c + 1) * 256)
                dst = slice(h * HALF + c * 256, h * HALF + (c + 1) * 256)
                nc.vector.quantize_mx(
                    out=zcode[:, g, dst].bitcast(FP8X4),
                    scales=zscale[:, g, dst],
                    in_=zi[:, cols, :].rearrange("p w j -> p (w j)"),
                )

        NEAR_FIRST = (0, 1, 2, 3)
        NEAR_LAST = (1, 2, 3, 0)

        def one_pass(n, order, i, c0=0, width=HALF):
            h, m = divmod(n, NT)
            g = order[i]
            mc = slice(m * P, (m + 1) * P)
            zc = slice(h * HALF + c0, h * HALF + c0 + width)
            if g == 0:
                lhsT, lhsT_scale = pcode[:, mc].bitcast(FP8X4), pscale[:, mc]
            else:
                lhsT = words[:, g - 1, 2 * m * P : 2 * (m + 1) * P].bitcast(FP4X4)
                lhsT_scale = fscale[:, g - 1, mc]
            nc.tensor.matmul_mx(
                out=sums[n][:, c0 : c0 + width],
                lhsT=lhsT,
                lhsT_scale=lhsT_scale,
                rhs=zcode[:, g, zc].bitcast(FP8X4),
                rhs_scale=zscale[:, g, zc],
                start=(i == 0),
                stop=(i == NG - 1),
            )

        sums = {}

        def open_tile(n):
            bank = psum.tile([P, 512], F32, name="bank")
            sums[n] = bank

        def whole_tile(n, order, parts=1):
            open_tile(n)
            width = HALF // parts
            for c in range(parts):
                for i in range(NG):
                    one_pass(n, order, i, c * width, width)

        def set_aside(n):
            rest = rpool.tile([P, HALF], F32, name="rest", align_bytes=64)
            nc.vector.tensor_copy(out=rest[:], in_=sums[n][:])
            sums[n] = rest

        logs = {}

        def log_part(n, c0=0, width=HALF):
            if c0 == 0:
                lnt = lpool.tile([P, HALF], F32, name="lnt", align_bytes=64)
                logs[n] = lnt
            nc.scalar.activation(out=logs[n][:, c0 : c0 + width], in_=sums[n][:, c0 : c0 + width], func=LN)

        def finish(n, parts=1):
            h, m = divmod(n, NT)
            res = opool.tile([P, HALF], F32, name="res", align_bytes=64)
            width = HALF // parts
            for c in range(parts):
                cols = slice(c * width, (c + 1) * width)
                oc = slice(h * HALF + c * width, h * HALF + (c + 1) * width)
                nc.vector.scalar_tensor_tensor(
                    out=res[:, cols], in0=logs[n][:, cols], scalar=disc[:, m : m + 1], in1=rew[:, m, oc], op0=ALU.mult, op1=ALU.add
                )
                nc.sync.dma_start(out=out[m * P : (m + 1) * P, oc], in_=res[:, cols])

        def drain(n):
            log_part(n)
            finish(n)

        turned = [turn_near(q, k) for q in range(2) for k in range(2)]
        nc.vector.tensor_copy(out=disc[:], in_=dbank[:, 0:NT])
        for k in range(2):
            group_near(0, k, turned[k])
        quantize_near(0)

        for n in range(4):
            open_tile(n)
        desirability(0, 0, 2)
        for n in range(4):
            one_pass(n, NEAR_FIRST, 0)
        for k in range(2):
            group_near(1, k, turned[2 + k])
        quantize_near(1)
        for n in range(4, FIRST):
            open_tile(n)
            one_pass(n, NEAR_FIRST, 0)
        for g in range(1, NG):
            desirability(g, 0, 1)
            for n in range(FIRST):
                one_pass(n, NEAR_FIRST, g)

        for n in range(FIRST):
            set_aside(n)
        for q in (2, 3):
            turned = [turn_near(q, k) for k in range(2)]
            for k in range(2):
                group_near(q, k, turned[k])
            quantize_near(q)
            if q == 2:
                whole_tile(FIRST, NEAR_LAST)
        for n in range(FIRST + 1, 13):
            whole_tile(n, NEAR_LAST)
        for g in range(NG):
            desirability(g, 1, 1)
        drain(7)
        for n in range(13, NT):
            whole_tile(n, NEAR_LAST)
        LAST = 2 * NT - 1
        for n in range(NT, 2 * NT):
            if n - NT < FIRST:
                drain(n - NT)
            drain(n - 8)
            whole_tile(n, NEAR_FIRST, 4 if n == LAST else 1)
        for n in range(LAST - 7, LAST):
            drain(n)
        for c in range(4):
            log_part(LAST, c * P, P)
        finish(LAST, 4)
